import numpy as np
import ml_dtypes


def mxq(x, axis, fmt="e4m3"):
    dtype, down = {"e4m3": (ml_dtypes.float8_e4m3fn, 7), "e5m2": (ml_dtypes.float8_e5m2, 14)}[fmt]
    v = np.moveaxis(np.asarray(x, np.float32).astype(ml_dtypes.bfloat16).astype(np.float64), axis, -1)
    blocks = v.reshape(v.shape[:-1] + (-1, 32))
    amax = np.abs(blocks).max(-1, keepdims=True)
    byte = np.maximum(np.where(amax > 0, np.frexp(amax)[1] - 1 + 127, 0) - down, 1)
    scale = np.exp2(byte - 127.0)
    codes = (blocks / scale).astype(np.float32).astype(dtype).astype(np.float64)
    return np.moveaxis((codes * scale).reshape(v.shape), -1, axis)


WIDE = False


def mx_kscale(k):
    if not WIDE:
        return np.ones(k)
    levels = np.array([10, -10, 5, -5, 0])
    if k % 512:
        return np.exp2(np.random.permutation(np.resize(levels, k // 32))).repeat(32)
    a = np.empty((k // 512, 16))
    for p in range(k // 512):
        a[p, :8] = np.random.permutation(np.resize(levels, 8))
        for g in range(8):
            far = levels[np.abs(levels - a[p, g]) >= 10]
            a[p, g + 8] = far[np.random.randint(len(far))]
    return np.exp2(a.ravel()).repeat(32)


def f64(x):
    return np.asarray(x).astype(np.float64)


def striped(idx):
    return np.tile(idx.reshape(-1, 16).T, (8, 1)).astype(np.uint16)


def unstriped(offs):
    return offs[:16].T.reshape(-1).astype(np.int64)


E2M1 = np.array([0.0, 0.5, 1.0, 1.5, 2.0, 3.0, 4.0, 6.0, -0.0, -0.5, -1.0, -1.5, -2.0, -3.0, -4.0, -6.0])


def pack_weight(w, fmt):
    k, n = w.shape
    w = f64(np.asarray(w, np.float32).astype(ml_dtypes.bfloat16)).reshape(k // 32, 32, n)
    amax = np.abs(w).max(1)
    if fmt == "e4m3":
        byte = np.frexp(amax)[1] - 1 + 127 - 7
    else:
        mant, ex = np.frexp(amax / 6.0)
        byte = np.where(mant > 0.5, ex, ex - 1) + 127
    byte = np.clip(np.where(amax > 0, byte, 1), 1, 254)
    scaled = (w * np.exp2(127.0 - byte)[:, None, :]).reshape(k, n).astype(np.float32)
    by_word = np.ascontiguousarray(scaled.reshape(k // 512, 128, 4, n).transpose(0, 1, 3, 2))
    if fmt == "e4m3":
        words = by_word.astype(ml_dtypes.float8_e4m3fn).view(np.uint8)
    else:
        c = by_word.astype(ml_dtypes.float4_e2m1fn).view(np.uint8) & 0xF
        words = (c[..., 0::2] | (c[..., 1::2] << 4)).reshape(k // 512, 128, 2 * n)
    return np.ascontiguousarray(words), np.ascontiguousarray(byte.astype(np.uint8).reshape(k // 512, 16, n))


def unpack_weight(words, scales, fmt):
    g, _, n = scales.shape
    words = np.ascontiguousarray(words).reshape(g, 128, n, -1)
    if fmt == "e4m3":
        vals = words.view(ml_dtypes.float8_e4m3fn).astype(np.float64)
    else:
        nib = np.empty((g, 128, n, 4), np.uint8)
        nib[..., 0::2] = words & 0xF
        nib[..., 1::2] = words >> 4
        vals = E2M1[nib]
    vals = vals * np.repeat(np.exp2(scales.astype(np.float64) - 127.0), 8, axis=1)[..., None]
    return vals.transpose(0, 1, 3, 2).reshape(g * 512, n)


def gelu(v):
    return 0.5 * v * (1.0 + np.tanh(np.sqrt(2.0 / np.pi) * (v + 0.044715 * v**3)))


def striped8(idx):
    return np.concatenate([v.reshape(-1, 16).T for v in idx]).astype(np.uint16)


def unstriped8(offs):
    return np.stack([offs[16 * g:16 * g + 16].T.reshape(-1) for g in range(8)]).astype(np.int64)


def runs(v, idx8):
    k = np.arange(v.shape[0])
    return v[k[:, None], idx8[k % 512 // 64]]


def often(T, S):
    return np.random.permutation(T)[(T * np.random.uniform(0, 1, S) ** 4).astype(np.int64)]


K, T, S, H, N = 1024, 2048, 512, 1024, 384

def setup_inputs():
    n = np.random.standard_normal
    s = mx_kscale(K)[:, None]
    u = mx_kscale(H)[:, None]
    tab_words, tab_scales = pack_weight(n((K, T)) * s, "e4m3")
    wdust_words, wdust_scales = pack_weight(n((K, H)) / np.sqrt(K) / s, "e2m1")
    wglow_words, wglow_scales = pack_weight(0.8 * n((K, N)) / np.sqrt(K) / s, "e4m3")
    return {
        "tab_words": tab_words, "tab_scales": tab_scales,
        "offs": striped8(np.stack([often(T, S) for _ in range(8)])),
        "wdust_words": wdust_words, "wdust_scales": wdust_scales,
        "bdust": (0.4 + 0.4 * n(H)).astype(np.float32),
        "wlight": (n((K, H)) / np.sqrt(K) / s * u.T).astype(np.float32),
        "wglow_words": wglow_words, "wglow_scales": wglow_scales,
        "wout": (1.5 * n((H, N)) / np.sqrt(H) / u).astype(np.float32),
    }

def reference(tab_words, tab_scales, offs, wdust_words, wdust_scales, bdust,
              wlight, wglow_words, wglow_scales, wout):
    v = runs(unpack_weight(tab_words, tab_scales, "e4m3"), unstriped8(offs))
    wdust = unpack_weight(wdust_words, wdust_scales, "e2m1")
    wglow = unpack_weight(wglow_words, wglow_scales, "e4m3")
    d = (wdust.T @ v) + f64(bdust)[:, None]
    depth = np.maximum(d, 0.0)
    light = mxq(f64(wlight), 0, "e4m3").T @ v
    h = np.exp(-depth) * light
    hq = mxq(h, 0, "e4m3")
    return mxq(f64(wout), 0, "e4m3").T @ hq + wglow.T @ v

@@ -1,0 +1,215 @@
+from contextlib import ExitStack
+
+import concourse.mybir as mybir
+from concourse.masks import make_identity
+
+K, T, S, H, N = 1024, 2048, 512, 1024, 384
+FLOPS = 2 * S * (K * H + K * H + H * N + K * N)
+
+F32 = mybir.dt.float32
+BF16 = mybir.dt.bfloat16
+I32 = mybir.dt.int32
+U32 = mybir.dt.uint32
+U16 = mybir.dt.uint16
+U8 = mybir.dt.uint8
+FP8X4 = mybir.dt.float8_e4m3fn_x4
+FP4X4 = mybir.dt.float4_e2m1fn_x4
+EXP = mybir.ActivationFunctionType.Exp
+COPY = mybir.ActivationFunctionType.Copy
+ALU = mybir.AluOpType
+
+P = 128
+PACK = 4
+PASS = P * PACK
+KP = K // PASS
+HP = H // PASS
+NT = N // P
+JC = S // P
+QUADS = 4
+SHIFT = 14
+LIVE = 100
+
+
+def tile_list_haze_sight_lines_kernel(tc, tab_words, tab_scales, offs, wdust_words, wdust_scales, bdust,
+                                               wlight, wglow_words, wglow_scales, wout, out):
+    nc = tc.nc
+    with ExitStack() as ctx:
+        keep = ctx.enter_context(tc.tile_pool(name="keep", bufs=1))
+        ring = ctx.enter_context(tc.tile_pool(name="ring", bufs=1))
+        psum = ctx.enter_context(tc.psum_pool(name="psum", bufs=1))
+
+        def staged(shape, dtype, name, slot):
+            return ring.tile(shape, dtype, name=name, tag=slot, align_bytes=64)
+
+        def bank(index, name):
+            return psum.tile([P, S], F32, name=name, tag="bank%d" % index)
+
+        offsets = keep.tile([P, S // 16], U16, name="offsets")
+        nc.sync.dma_start(offsets[:], offs)
+
+        tsc = staged([P, KP * T], U8, "tsc", "A")
+        nc.vector.memset(tsc[:].bitcast(I32), 0)
+        dsc_raw = staged([P, KP * H], U8, "dsc_raw", "Y")
+        nc.gpsimd.memset(dsc_raw[:].bitcast(I32), 0)
+        braw = keep.tile([P, P], F32, name="braw")
+        nc.vector.memset(braw[:], 0.0)
+        vsc = keep.tile([P, KP * S], U8, name="vsc", align_bytes=64)
+        nc.vector.memset(vsc[:].bitcast(I32), 0)
+
+        for d in range(QUADS):
+            nc.scalar.dma_start(
+                tsc[32 * d + SHIFT: 32 * d + SHIFT + 4, :].bitcast(I32).rearrange("q (a t) -> q a t", a=KP),
+                tab_scales[:, 4 * d: 4 * d + 4, :].rearrange("a q t -> q a t").bitcast(I32))
+        brows = bdust.rearrange("(b g t i) -> b t g i", b=HP, t=PACK, i=4)
+        for b in range(HP):
+            nc.scalar.dma_start(braw[PACK * b: PACK * (b + 1), :].rearrange("t (g i) -> t g i", i=4), brows[b])
+        tsc1 = staged([P, T], U8, "tsc1", "X")
+        tab = [staged([P, T], I32, "tab0", "B")]
+        nc.sync.dma_start(tab[0][:], tab_words[0].rearrange("p t i -> p (t i)").bitcast(I32))
+        for d in range(QUADS):
+            nc.gpsimd.dma_start(
+                dsc_raw[32 * d: 32 * d + 4, :].bitcast(I32).rearrange("q (a c) -> q a c", a=KP),
+                wdust_scales[:, 4 * d: 4 * d + 4, :].rearrange("a q c -> q a c").bitcast(I32))
+        dw_raw = staged([P, KP, H // 2], I32, "dw_raw", "C")
+        nc.sync.dma_start(dw_raw[:], wdust_words.rearrange("a p c -> p a c").bitcast(I32))
+
+        ident = keep.tile([P, P], F32, name="ident")
+        make_identity(nc, ident[:])
+        picked = staged([P, KP * S], U8, "picked", "D")
+        nc.vector.tensor_copy(picked[:, 0:S], tsc[:].indirect(offsets[:]))
+        nc.vector.tensor_copy(tsc1[:].bitcast(I32), tsc[:, T: 2 * T].bitcast(I32))
+        tab.append(staged([P, T], I32, "tab1", "A"))
+        nc.sync.dma_start(tab[1][:], tab_words[1].rearrange("p t i -> p (t i)").bitcast(I32))
+        nc.vector.tensor_copy(picked[:, S: 2 * S], tsc1[:].indirect(offsets[:]))
+        nc.scalar.dma_start(vsc[0:LIVE, :].bitcast(I32), picked[SHIFT: SHIFT + LIVE, :].bitcast(I32))
+
+        gsc = keep.tile([P, KP * N], U8, name="gsc", align_bytes=64)
+        nc.gpsimd.memset(gsc[:].bitcast(I32), 0)
+        for d in range(QUADS):
+            nc.gpsimd.dma_start(
+                gsc[32 * d: 32 * d + 4, :].bitcast(I32).rearrange("q (a c) -> q a c", a=KP),
+                wglow_scales[:, 4 * d: 4 * d + 4, :].rearrange("a q c -> q a c").bitcast(I32))
+
+        wd = staged([P, 3 * KP * H], U8, "wd", "X")
+        dw = wd[:, 0: 2 * KP * H]
+        dsc = wd[:, 2 * KP * H: 3 * KP * H]
+        nc.vector.tensor_copy(
+            dsc.bitcast(I32).rearrange("p (u t c i) -> p u c t i", u=KP * HP, t=PACK, i=4),
+            dsc_raw[:].bitcast(I32).rearrange("p (u c i t) -> p u c t i", u=KP * HP, t=PACK, i=4))
+        nc.vector.tensor_copy(
+            dw.bitcast(I32).rearrange("p (u t g w) -> p u t g w", u=KP * HP, t=PACK, w=2),
+            dw_raw[:].rearrange("p a (b g t w) -> p (a b) t g w", b=HP, t=PACK, w=2))
+        v = [staged([P, S], U32, "v0", "Y"), keep.tile([P, S], U32, name="v1", align_bytes=64)]
+        for a in range(KP):
+            nc.vector.tensor_copy(v[a][:], tab[a][:].bitcast(U32).indirect(offsets[:]))
+        nbias = keep.tile([P, HP, PACK], F32, name="nbias")
+        turned = bank(HP * PACK - 1, "turned")
+        nc.tensor.transpose(turned[:, 0:P], braw[:], ident[:])
+        nc.scalar.activation(nbias[:].rearrange("p b t -> p (b t)"), turned[:, 0: HP * PACK], COPY, scale=-1.0)
+
+        e = []
+        for b in range(HP):
+            eb = keep.tile([P, PACK, S], F32, name="e%d" % b)
+            e.append(eb)
+            for t in range(PACK):
+                acc = bank(PACK * b + t, "d%d%d" % (b, t))
+                for a in range(KP):
+                    c0 = a * H + b * PASS + t * P
+                    nc.tensor.matmul_mx(acc[:], lhsT=dw[:, 2 * c0: 2 * (c0 + P)].bitcast(FP4X4),
+                                        lhsT_scale=dsc[:, c0: c0 + P],
+                                        rhs=v[a][:].bitcast(FP8X4), rhs_scale=vsc[:, a * S: (a + 1) * S],
+                                        start=(a == 0), stop=(a == KP - 1))
+                nc.scalar.activation(eb[:, t, :], acc[:], EXP, bias=nbias[:, b, t: t + 1], scale=-1.0)
+
+        def load_wlight(a, b, slot):
+            raw = staged([P, PACK, PASS], F32, "wl%d%d" % (a, b), slot)
+            nc.sync.dma_start(raw[:], wlight[a * PASS: (a + 1) * PASS, b * PASS: (b + 1) * PASS]
+                              .rearrange("(p j) c -> p j c", j=PACK))
+            return raw[:].rearrange("p j (g t i) -> p t g j i", t=PACK, i=4)
+
+        def cast_half(src, half, copy, name):
+            grouped = keep.tile([P, 2 * PASS], BF16, name=name, align_bytes=64)
+            copy(grouped[:].rearrange("p (t g i j) -> p t g j i", t=2, i=4, j=PACK), src[:, 2 * half: 2 * half + 2])
+            return grouped
+
+        def quantise(grouped, width, name):
+            codes = keep.tile([P, width], U32, name=name + "c", align_bytes=64)
+            scales = keep.tile([P, width], U8, name=name + "s", align_bytes=64)
+            nc.vector.quantize_mx(codes[:].bitcast(FP8X4), scales[:], grouped[:])
+            return codes, scales
+
+        def light_passes(lights, a, quant):
+            for jc in range(JC):
+                for t in range(PACK):
+                    codes, scales = quant[t // 2]
+                    m = slice((t % 2) * P, (t % 2 + 1) * P)
+                    nc.tensor.matmul_mx(lights[jc][:, t * P: (t + 1) * P], lhsT=codes[:, m].bitcast(FP8X4),
+                                        lhsT_scale=scales[:, m],
+                                        rhs=v[a][:, jc * P: (jc + 1) * P].bitcast(FP8X4),
+                                        rhs_scale=vsc[:, a * S + jc * P: a * S + (jc + 1) * P],
+                                        start=(a == 0 and t == 0), stop=(a == KP - 1 and t == PACK - 1))
+
+        def dim(b, jc, light):
+            h = keep.tile([P, PASS], BF16, name="h%d%d" % (b, jc), align_bytes=64)
+            nc.vector.scalar_tensor_tensor(
+                h[:].rearrange("p (j t) -> p j t", t=PACK),
+                e[b][:, :, jc * P: (jc + 1) * P].rearrange("p t j -> p j t"), 1.0,
+                light[:].rearrange("p (t j) -> p j t", t=PACK), ALU.min, ALU.mult)
+            return h
+
+        on_vector, on_scalar = nc.vector.tensor_copy, nc.scalar.copy
+        copiers = {(0, 0): (on_vector, on_vector), (1, 0): (on_vector, on_vector),
+                   (0, 1): (on_scalar, on_scalar), (1, 1): (on_vector, on_scalar)}
+        slots = {(0, 0): "C", (1, 0): "B", (0, 1): "A", (1, 1): "D"}
+        hq = {}
+        wo = []
+        for b in range(HP):
+            lights = [bank(JC * b + jc, "l%d%d" % (b, jc)) for jc in range(JC)]
+            for a in range(KP):
+                src = load_wlight(a, b, slots[(a, b)])
+                halves = [cast_half(src, half, copiers[(a, b)][half], "wl%d%d%d" % (a, b, half)) for half in range(2)]
+                quant = [quantise(halves[half], 2 * P, "wl%d%d%d" % (a, b, half)) for half in range(2)]
+                light_passes(lights, a, quant)
+            hb = []
+            for jc in range(JC + 1):
+                if jc < JC:
+                    hb.append(dim(b, jc, lights[jc]))
+                if jc > 0:
+                    hq[(b, jc - 1)] = quantise(hb[jc - 1], P, "h%d%d" % (b, jc - 1))
+
+        for b in range(HP):
+            raw = staged([P, PACK, N], F32, "wo%d" % b, "CB"[b])
+            rows = wout[b * PASS: (b + 1) * PASS, :].rearrange("(g t i) n -> t g i n", t=PACK, i=4)
+            for t in range(PACK):
+                nc.sync.dma_start(raw[:, t, :], rows[t])
+            parts = []
+            for n in range(NT):
+                grouped = keep.tile([P, PASS], BF16, name="wog%d%d" % (b, n), align_bytes=64)
+                nc.scalar.copy(grouped[:].rearrange("p (c i t) -> p c t i", i=4, t=PACK),
+                               raw[:, :, n * P: (n + 1) * P].rearrange("p t (c i) -> p c t i", i=4))
+                parts.append(quantise(grouped, P, "wo%d%d" % (b, n)))
+            wo.append(parts)
+
+        gw = staged([P, KP, N], I32, "gw", "A")
+        nc.sync.dma_start(gw[:], wglow_words.rearrange("a p c i -> p a (c i)").bitcast(I32))
+
+        out_rows = out.rearrange("(n p) j -> p n j", p=P)
+        for jc in range(JC):
+            cols = slice(jc * P, (jc + 1) * P)
+            acc = bank(jc, "o%d" % jc)
+            passes = []
+            for n in range(NT):
+                passes.append((n, wo[0][n][0][:], wo[0][n][1][:], hq[(0, jc)][0][:], hq[(0, jc)][1][:]))
+            for a in range(KP):
+                for n in range(NT):
+                    passes.append((n, gw[:, a, n * P: (n + 1) * P], gsc[:, a * N + n * P: a * N + (n + 1) * P],
+                                   v[a][:, cols], vsc[:, a * S + jc * P: a * S + (jc + 1) * P]))
+            for n in range(NT):
+                passes.append((n, wo[1][n][0][:], wo[1][n][1][:], hq[(1, jc)][0][:], hq[(1, jc)][1][:]))
+            for index, (n, lhs, lhs_scale, rhs, rhs_scale) in enumerate(passes):
+                nc.tensor.matmul_mx(acc[:, n * P: (n + 1) * P], lhsT=lhs.bitcast(FP8X4), lhsT_scale=lhs_scale,
+                                    rhs=rhs.bitcast(FP8X4), rhs_scale=rhs_scale,
+                                    start=(index == 0), stop=(index == len(passes) - 1))
+            result = keep.tile([P, NT, P], F32, name="res%d" % jc)
+            nc.scalar.copy(result[:].rearrange("p n j -> p (n j)"), acc[:, 0:N])
+            nc.sync.dma_start(out_rows[:, :, cols], result[:])

@@ -26,8 +26,7 @@ HP = H // PASS
 NT = N // P
 JC = S // P
 QUADS = 4
-SHIFT = 14
-LIVE = 100
+ROW = S + H + N
 
 
 def tile_list_haze_sight_lines_kernel(tc, tab_words, tab_scales, offs, wdust_words, wdust_scales, bdust,
@@ -47,77 +46,67 @@ def tile_list_haze_sight_lines_kernel(tc, tab_words, tab_scales, offs, wdust_wor
         offsets = keep.tile([P, S // 16], U16, name="offsets")
         nc.sync.dma_start(offsets[:], offs)
 
-        tsc = staged([P, KP * T], U8, "tsc", "A")
+        tsc = staged([P, T], U8, "tsc", "X")
         nc.vector.memset(tsc[:].bitcast(I32), 0)
-        dsc_raw = staged([P, KP * H], U8, "dsc_raw", "Y")
-        nc.gpsimd.memset(dsc_raw[:].bitcast(I32), 0)
+        dsc_raw = keep.tile([P, H], U8, name="dsc_raw", align_bytes=64)
+        nc.vector.memset(dsc_raw[:].bitcast(I32), 0)
+        rows4 = staged([P, ROW], U8, "rows4", "D")
+        nc.gpsimd.memset(rows4[:, S + H: ROW].bitcast(I32), 0)
         braw = keep.tile([P, P], F32, name="braw")
-        nc.vector.memset(braw[:], 0.0)
-        vsc = keep.tile([P, KP * S], U8, name="vsc", align_bytes=64)
-        nc.vector.memset(vsc[:].bitcast(I32), 0)
+        nc.gpsimd.memset(braw[:], 0.0)
+        planes = keep.tile([P, KP * ROW], U8, name="planes", align_bytes=64)
+        nc.vector.memset(planes[:].bitcast(I32), 0)
 
-        for d in range(QUADS):
-            nc.scalar.dma_start(
-                tsc[32 * d + SHIFT: 32 * d + SHIFT + 4, :].bitcast(I32).rearrange("q (a t) -> q a t", a=KP),
-                tab_scales[:, 4 * d: 4 * d + 4, :].rearrange("a q t -> q a t").bitcast(I32))
+        nc.scalar.dma_start(tsc[0:P:4, :].bitcast(I32), tab_scales.rearrange("a q t -> q a t").bitcast(I32))
+        nc.scalar.dma_start(dsc_raw[0:P:4, :].bitcast(I32), wdust_scales.rearrange("a q c -> q a c").bitcast(I32))
+        nc.gpsimd.dma_start(rows4[0:P:4, S + H: ROW].bitcast(I32),
+                            wglow_scales.rearrange("a q c -> q a c").bitcast(I32))
+        tab = [staged([P, T], I32, "tab%d" % a, "BA"[a]) for a in range(KP)]
+        dw_raw = keep.tile([P, KP, H // 2], I32, name="dw_raw", align_bytes=64)
+        nc.sync.dma_start(tab[0][:], tab_words[0].rearrange("p t i -> p (t i)").bitcast(I32))
+        nc.sync.dma_start(dw_raw[:], wdust_words.rearrange("a p c -> p a c").bitcast(I32))
+        nc.sync.dma_start(tab[1][:], tab_words[1].rearrange("p t i -> p (t i)").bitcast(I32))
         brows = bdust.rearrange("(b g t i) -> b t g i", b=HP, t=PACK, i=4)
         for b in range(HP):
-            nc.scalar.dma_start(braw[PACK * b: PACK * (b + 1), :].rearrange("t (g i) -> t g i", i=4), brows[b])
-        tsc1 = staged([P, T], U8, "tsc1", "X")
-        tab = [staged([P, T], I32, "tab0", "B")]
-        nc.sync.dma_start(tab[0][:], tab_words[0].rearrange("p t i -> p (t i)").bitcast(I32))
-        for d in range(QUADS):
-            nc.gpsimd.dma_start(
-                dsc_raw[32 * d: 32 * d + 4, :].bitcast(I32).rearrange("q (a c) -> q a c", a=KP),
-                wdust_scales[:, 4 * d: 4 * d + 4, :].rearrange("a q c -> q a c").bitcast(I32))
-        dw_raw = staged([P, KP, H // 2], I32, "dw_raw", "C")
-        nc.sync.dma_start(dw_raw[:], wdust_words.rearrange("a p c -> p a c").bitcast(I32))
-
+            nc.gpsimd.dma_start(braw[PACK * b: PACK * (b + 1), :].rearrange("t (g i) -> t g i", i=4), brows[b])
         ident = keep.tile([P, P], F32, name="ident")
         make_identity(nc, ident[:])
-        picked = staged([P, KP * S], U8, "picked", "D")
-        nc.vector.tensor_copy(picked[:, 0:S], tsc[:].indirect(offsets[:]))
-        nc.vector.tensor_copy(tsc1[:].bitcast(I32), tsc[:, T: 2 * T].bitcast(I32))
-        tab.append(staged([P, T], I32, "tab1", "A"))
-        nc.sync.dma_start(tab[1][:], tab_words[1].rearrange("p t i -> p (t i)").bitcast(I32))
-        nc.vector.tensor_copy(picked[:, S: 2 * S], tsc1[:].indirect(offsets[:]))
-        nc.scalar.dma_start(vsc[0:LIVE, :].bitcast(I32), picked[SHIFT: SHIFT + LIVE, :].bitcast(I32))
 
-        gsc = keep.tile([P, KP * N], U8, name="gsc", align_bytes=64)
-        nc.gpsimd.memset(gsc[:].bitcast(I32), 0)
+        picked = keep.tile([P, S], U8, name="picked", align_bytes=64)
+        nc.vector.tensor_copy(picked[:], tsc[:].indirect(offsets[:]))
+        nc.vector.tensor_copy(
+            rows4[:, S: S + H].bitcast(I32).rearrange("p (b t c i) -> p b c t i", b=HP, t=PACK, i=4),
+            dsc_raw[:].bitcast(I32).rearrange("p (b c i t) -> p b c t i", b=HP, t=PACK, i=4))
+        nc.vector.tensor_copy(rows4[:, 0:S].bitcast(I32), picked[:].bitcast(I32))
         for d in range(QUADS):
-            nc.gpsimd.dma_start(
-                gsc[32 * d: 32 * d + 4, :].bitcast(I32).rearrange("q (a c) -> q a c", a=KP),
-                wglow_scales[:, 4 * d: 4 * d + 4, :].rearrange("a q c -> q a c").bitcast(I32))
+            nc.scalar.dma_start(
+                planes[32 * d: 32 * d + 4, :].bitcast(I32).rearrange("q (a j) -> q a j", a=KP),
+                rows4[32 * d: 32 * (d + 1): 4, :].bitcast(I32))
 
-        wd = staged([P, 3 * KP * H], U8, "wd", "X")
-        dw = wd[:, 0: 2 * KP * H]
-        dsc = wd[:, 2 * KP * H: 3 * KP * H]
+        v = [staged([P, S], U32, "v0", "X"), keep.tile([P, S], U32, name="v1", align_bytes=64)]
+        nc.vector.tensor_copy(v[0][:], tab[0][:].bitcast(U32).indirect(offsets[:]))
+        dw = staged([P, 2 * KP * H], U8, "dw", "B")
         nc.vector.tensor_copy(
-            dsc.bitcast(I32).rearrange("p (u t c i) -> p u c t i", u=KP * HP, t=PACK, i=4),
-            dsc_raw[:].bitcast(I32).rearrange("p (u c i t) -> p u c t i", u=KP * HP, t=PACK, i=4))
-        nc.vector.tensor_copy(
-            dw.bitcast(I32).rearrange("p (u t g w) -> p u t g w", u=KP * HP, t=PACK, w=2),
+            dw[:].bitcast(I32).rearrange("p (u t g w) -> p u t g w", u=KP * HP, t=PACK, w=2),
             dw_raw[:].rearrange("p a (b g t w) -> p (a b) t g w", b=HP, t=PACK, w=2))
-        v = [staged([P, S], U32, "v0", "Y"), keep.tile([P, S], U32, name="v1", align_bytes=64)]
-        for a in range(KP):
-            nc.vector.tensor_copy(v[a][:], tab[a][:].bitcast(U32).indirect(offsets[:]))
-        nbias = keep.tile([P, HP, PACK], F32, name="nbias")
+        nc.vector.tensor_copy(v[1][:], tab[1][:].bitcast(U32).indirect(offsets[:]))
+        nbias = staged([P, HP, PACK], F32, "nbias", "nbias")
         turned = bank(HP * PACK - 1, "turned")
         nc.tensor.transpose(turned[:, 0:P], braw[:], ident[:])
         nc.scalar.activation(nbias[:].rearrange("p b t -> p (b t)"), turned[:, 0: HP * PACK], COPY, scale=-1.0)
 
         e = []
         for b in range(HP):
-            eb = keep.tile([P, PACK, S], F32, name="e%d" % b)
+            eb = staged([P, PACK, S], F32, "e%d" % b, "e%d" % b)
             e.append(eb)
             for t in range(PACK):
                 acc = bank(PACK * b + t, "d%d%d" % (b, t))
                 for a in range(KP):
                     c0 = a * H + b * PASS + t * P
+                    s0 = a * ROW + S + b * PASS + t * P
                     nc.tensor.matmul_mx(acc[:], lhsT=dw[:, 2 * c0: 2 * (c0 + P)].bitcast(FP4X4),
-                                        lhsT_scale=dsc[:, c0: c0 + P],
-                                        rhs=v[a][:].bitcast(FP8X4), rhs_scale=vsc[:, a * S: (a + 1) * S],
+                                        lhsT_scale=planes[:, s0: s0 + P],
+                                        rhs=v[a][:].bitcast(FP8X4), rhs_scale=planes[:, a * ROW: a * ROW + S],
                                         start=(a == 0), stop=(a == KP - 1))
                 nc.scalar.activation(eb[:, t, :], acc[:], EXP, bias=nbias[:, b, t: t + 1], scale=-1.0)
 
@@ -127,16 +116,13 @@ def tile_list_haze_sight_lines_kernel(tc, tab_words, tab_scales, offs, wdust_wor
                               .rearrange("(p j) c -> p j c", j=PACK))
             return raw[:].rearrange("p j (g t i) -> p t g j i", t=PACK, i=4)
 
-        def cast_half(src, half, copy, name):
-            grouped = keep.tile([P, 2 * PASS], BF16, name=name, align_bytes=64)
-            copy(grouped[:].rearrange("p (t g i j) -> p t g j i", t=2, i=4, j=PACK), src[:, 2 * half: 2 * half + 2])
-            return grouped
+        def cast_half(grouped, src, half, copy):
+            copy(grouped.rearrange("p (t g i j) -> p t g j i", t=2, i=4, j=PACK), src[:, 2 * half: 2 * half + 2])
 
-        def quantise(grouped, width, name):
-            codes = keep.tile([P, width], U32, name=name + "c", align_bytes=64)
-            scales = keep.tile([P, width], U8, name=name + "s", align_bytes=64)
-            nc.vector.quantize_mx(codes[:].bitcast(FP8X4), scales[:], grouped[:])
-            return codes, scales
+        def quantise(grouped, codes, name):
+            scales = keep.tile([P, codes.shape[1]], U8, name=name, align_bytes=64)
+            nc.vector.quantize_mx(codes.bitcast(FP8X4), scales[:], grouped)
+            return codes, scales[:]
 
         def light_passes(lights, a, quant):
             for jc in range(JC):
@@ -146,11 +132,11 @@ def tile_list_haze_sight_lines_kernel(tc, tab_words, tab_scales, offs, wdust_wor
                     nc.tensor.matmul_mx(lights[jc][:, t * P: (t + 1) * P], lhsT=codes[:, m].bitcast(FP8X4),
                                         lhsT_scale=scales[:, m],
                                         rhs=v[a][:, jc * P: (jc + 1) * P].bitcast(FP8X4),
-                                        rhs_scale=vsc[:, a * S + jc * P: a * S + (jc + 1) * P],
+                                        rhs_scale=planes[:, a * ROW + jc * P: a * ROW + (jc + 1) * P],
                                         start=(a == 0 and t == 0), stop=(a == KP - 1 and t == PACK - 1))
 
         def dim(b, jc, light):
-            h = keep.tile([P, PASS], BF16, name="h%d%d" % (b, jc), align_bytes=64)
+            h = staged([P, PASS], BF16, "h%d%d" % (b, jc), "h%d%d" % (b, jc))
             nc.vector.scalar_tensor_tensor(
                 h[:].rearrange("p (j t) -> p j t", t=PACK),
                 e[b][:, :, jc * P: (jc + 1) * P].rearrange("p t j -> p j t"), 1.0,
@@ -158,58 +144,87 @@ def tile_list_haze_sight_lines_kernel(tc, tab_words, tab_scales, offs, wdust_wor
             return h
 
         on_vector, on_scalar = nc.vector.tensor_copy, nc.scalar.copy
-        copiers = {(0, 0): (on_vector, on_vector), (1, 0): (on_vector, on_vector),
-                   (0, 1): (on_scalar, on_scalar), (1, 1): (on_vector, on_scalar)}
-        slots = {(0, 0): "C", (1, 0): "B", (0, 1): "A", (1, 1): "D"}
-        hq = {}
-        wo = []
-        for b in range(HP):
-            lights = [bank(JC * b + jc, "l%d%d" % (b, jc)) for jc in range(JC)]
-            for a in range(KP):
-                src = load_wlight(a, b, slots[(a, b)])
-                halves = [cast_half(src, half, copiers[(a, b)][half], "wl%d%d%d" % (a, b, half)) for half in range(2)]
-                quant = [quantise(halves[half], 2 * P, "wl%d%d%d" % (a, b, half)) for half in range(2)]
-                light_passes(lights, a, quant)
-            hb = []
-            for jc in range(JC + 1):
-                if jc < JC:
-                    hb.append(dim(b, jc, lights[jc]))
-                if jc > 0:
-                    hq[(b, jc - 1)] = quantise(hb[jc - 1], P, "h%d%d" % (b, jc - 1))
 
+        def own(shape, dtype, name):
+            return staged(shape, dtype, name, name)[:]
+
+        lights0 = [bank(jc, "l0%d" % jc) for jc in range(JC)]
+        for a in range(KP):
+            src = load_wlight(a, 0, "CD"[a])
+            halves = [own([P, 2 * PASS], BF16, "g%d0%d" % (a, half)) for half in range(2)]
+            for half in range(2):
+                cast_half(halves[half], src, half, on_vector)
+            light_passes(lights0, a, [quantise(halves[half], own([P, 2 * P], U32, "c%d0%d" % (a, half)),
+                                               "s%d0%d" % (a, half)) for half in range(2)])
+        lights1 = [bank(JC + jc, "l1%d" % jc) for jc in range(JC)]
+        src = load_wlight(0, 1, "A")
+        g01 = staged([P, PACK * PASS], BF16, "g01", "nbias")
+        for half in range(2):
+            cast_half(g01[:, 2 * PASS * half: 2 * PASS * (half + 1)], src, half, on_scalar)
+        src11 = load_wlight(1, 1, "C")
+        g111 = own([P, 2 * PASS], BF16, "g111")
+        cast_half(g111, src11, 1, on_scalar)
+
+        h0 = [dim(0, jc, lights0[jc]) for jc in range(JC)]
+        hq0 = [quantise(h0[jc][:], own([P, P], U32, "hc0%d" % jc), "hs0%d" % jc) for jc in range(JC)]
+        light_passes(lights1, 0, [quantise(g01[:, 2 * PASS * half: 2 * PASS * (half + 1)],
+                                           staged([P, 2 * P], U32, "c01%d" % half, "h0%d" % (2 + half))[:],
+                                           "s01%d" % half) for half in range(2)])
+        g110 = staged([P, 2 * PASS], BF16, "g110", "e0")[:]
+        cast_half(g110, src11, 0, on_vector)
+        q111 = quantise(g111, own([P, 2 * P], U32, "c111"), "s111")
+        q110 = quantise(g110, own([P, 2 * P], U32, "c110"), "s110")
+        light_passes(lights1, 1, [q110, q111])
+
+        rows = wout.rearrange("(b g t i) n -> b t g i n", b=HP, t=PACK, i=4)
+        wo_bf = staged([P, HP * NT * PASS], BF16, "wo_bf", "A")
         for b in range(HP):
-            raw = staged([P, PACK, N], F32, "wo%d" % b, "CB"[b])
-            rows = wout[b * PASS: (b + 1) * PASS, :].rearrange("(g t i) n -> t g i n", t=PACK, i=4)
+            wo_raw = staged([P, PACK, N], F32, "wo_raw%d" % b, ("D", "g100")[b])
             for t in range(PACK):
-                nc.sync.dma_start(raw[:, t, :], rows[t])
-            parts = []
+                nc.sync.dma_start(wo_raw[:, t, :], rows[b, t])
             for n in range(NT):
-                grouped = keep.tile([P, PASS], BF16, name="wog%d%d" % (b, n), align_bytes=64)
-                nc.scalar.copy(grouped[:].rearrange("p (c i t) -> p c t i", i=4, t=PACK),
-                               raw[:, :, n * P: (n + 1) * P].rearrange("p t (c i) -> p c t i", i=4))
-                parts.append(quantise(grouped, P, "wo%d%d" % (b, n)))
-            wo.append(parts)
-
-        gw = staged([P, KP, N], I32, "gw", "A")
+                u = NT * b + n
+                nc.scalar.copy(wo_bf[:, u * PASS: (u + 1) * PASS].rearrange("p (c i t) -> p c t i", i=4, t=PACK),
+                               wo_raw[:, :, n * P: (n + 1) * P].rearrange("p t (c i) -> p c t i", i=4))
+        gw = staged([P, KP, N], I32, "gw", "g101")
         nc.sync.dma_start(gw[:], wglow_words.rearrange("a p c i -> p a (c i)").bitcast(I32))
 
-        out_rows = out.rearrange("(n p) j -> p n j", p=P)
+        def quantise_wout(b, slot):
+            codes = staged([P, N], U32, "woc%d" % b, slot)
+            return [quantise(wo_bf[:, (NT * b + n) * PASS: (NT * b + n + 1) * PASS], codes[:, n * P: (n + 1) * P],
+                             "wos%d%d" % (b, n)) for n in range(NT)]
+
+        def quantise_h1(jc):
+            return quantise(h1[jc][:], own([P, P], U32, "hc1%d" % jc), "hs1%d" % jc)
+
+        h1 = [dim(1, 0, lights1[0]), dim(1, 1, lights1[1])]
+        wo = quantise_wout(0, "e0")
+        hq1 = [quantise_h1(0)]
+        h1.append(dim(1, 2, lights1[2]))
+        hq1.append(quantise_h1(1))
+        wo.extend(quantise_wout(1, "h10"))
+        h1.append(dim(1, 3, lights1[3]))
+        hq1.extend([quantise_h1(jc) for jc in (2, 3)])
+
+        sums = [bank(jc, "o%d" % jc) for jc in range(JC)]
+
+        def out_pass(jc, n, lhs, lhs_scale, rhs, rhs_scale, start, stop):
+            nc.tensor.matmul_mx(sums[jc][:, n * P: (n + 1) * P], lhsT=lhs.bitcast(FP8X4), lhsT_scale=lhs_scale,
+                                rhs=rhs.bitcast(FP8X4), rhs_scale=rhs_scale, start=start, stop=stop)
+
         for jc in range(JC):
-            cols = slice(jc * P, (jc + 1) * P)
-            acc = bank(jc, "o%d" % jc)
-            passes = []
             for n in range(NT):
-                passes.append((n, wo[0][n][0][:], wo[0][n][1][:], hq[(0, jc)][0][:], hq[(0, jc)][1][:]))
+                out_pass(jc, n, wo[n][0], wo[n][1], hq0[jc][0], hq0[jc][1], n == 0, False)
+        for jc in range(JC):
             for a in range(KP):
                 for n in range(NT):
-                    passes.append((n, gw[:, a, n * P: (n + 1) * P], gsc[:, a * N + n * P: a * N + (n + 1) * P],
-                                   v[a][:, cols], vsc[:, a * S + jc * P: a * S + (jc + 1) * P]))
+                    out_pass(jc, n, gw[:, a, n * P: (n + 1) * P], planes[:, a * ROW + S + H + n * P: a * ROW + S + H + (n + 1) * P],
+                             v[a][:, jc * P: (jc + 1) * P], planes[:, a * ROW + jc * P: a * ROW + (jc + 1) * P], False, False)
+        out_rows = out.rearrange("(n p) j -> p n j", p=P)
+        for jc in range(JC):
             for n in range(NT):
-                passes.append((n, wo[1][n][0][:], wo[1][n][1][:], hq[(1, jc)][0][:], hq[(1, jc)][1][:]))
-            for index, (n, lhs, lhs_scale, rhs, rhs_scale) in enumerate(passes):
-                nc.tensor.matmul_mx(acc[:, n * P: (n + 1) * P], lhsT=lhs.bitcast(FP8X4), lhsT_scale=lhs_scale,
-                                    rhs=rhs.bitcast(FP8X4), rhs_scale=rhs_scale,
-                                    start=(index == 0), stop=(index == len(passes) - 1))
+                out_pass(jc, n, wo[NT + n][0], wo[NT + n][1], hq1[jc][0], hq1[jc][1], False, n == NT - 1)
             result = keep.tile([P, NT, P], F32, name="res%d" % jc)
-            nc.scalar.copy(result[:].rearrange("p n j -> p (n j)"), acc[:, 0:N])
-            nc.sync.dma_start(out_rows[:, :, cols], result[:])
+            evacuate = on_vector if jc == JC - 1 else on_scalar
+            evacuate(result[:].rearrange("p n j -> p (n j)"), sums[jc][:, 0:N])
+            nc.sync.dma_start(out_rows[:, :, jc * P: (jc + 1) * P], result[:])

@@ -21,12 +21,17 @@ ALU = mybir.AluOpType
 P = 128
 PACK = 4
 PASS = P * PACK
+RUN = 4
 KP = K // PASS
 HP = H // PASS
 NT = N // P
 JC = S // P
-QUADS = 4
-ROW = S + H + N
+QUAD = 32
+QUADS = P // QUAD
+BLOCKS = 4
+ROW_STEP = 4
+ROW = S + H
+HALF = PASS // 2
 
 
 def tile_list_haze_sight_lines_kernel(tc, tab_words, tab_scales, offs, wdust_words, wdust_scales, bdust,
@@ -34,197 +39,211 @@ def tile_list_haze_sight_lines_kernel(tc, tab_words, tab_scales, offs, wdust_wor
     nc = tc.nc
     with ExitStack() as ctx:
         keep = ctx.enter_context(tc.tile_pool(name="keep", bufs=1))
-        ring = ctx.enter_context(tc.tile_pool(name="ring", bufs=1))
+        shared = ctx.enter_context(tc.tile_pool(name="shared", bufs=1))
         psum = ctx.enter_context(tc.psum_pool(name="psum", bufs=1))
 
-        def staged(shape, dtype, name, slot):
-            return ring.tile(shape, dtype, name=name, tag=slot, align_bytes=64)
+        def in_slot(slot, shape, dtype, name):
+            return shared.tile(shape, dtype, name=name, tag=slot, align_bytes=64)[:]
+
+        def new_slot(shape, dtype, name):
+            return in_slot(name, shape, dtype, name)
 
         def bank(index, name):
-            return psum.tile([P, S], F32, name=name, tag="bank%d" % index)
+            return psum.tile([P, S], F32, name=name, tag="bank%d" % index)[:]
 
         offsets = keep.tile([P, S // 16], U16, name="offsets")
         nc.sync.dma_start(offsets[:], offs)
 
-        tsc = staged([P, T], U8, "tsc", "X")
-        nc.vector.memset(tsc[:].bitcast(I32), 0)
-        dsc_raw = keep.tile([P, H], U8, name="dsc_raw", align_bytes=64)
-        nc.vector.memset(dsc_raw[:].bitcast(I32), 0)
-        rows4 = staged([P, ROW], U8, "rows4", "D")
-        nc.gpsimd.memset(rows4[:, S + H: ROW].bitcast(I32), 0)
-        braw = keep.tile([P, P], F32, name="braw")
-        nc.gpsimd.memset(braw[:], 0.0)
-        planes = keep.tile([P, KP * ROW], U8, name="planes", align_bytes=64)
-        nc.vector.memset(planes[:].bitcast(I32), 0)
+        tab_rows = new_slot([P, T], U8, "tab_rows")
+        nc.vector.memset(tab_rows.bitcast(I32), 0)
+        dust_rows = new_slot([P, H], U8, "dust_rows")
+        nc.vector.memset(dust_rows.bitcast(I32), 0)
+        bias_rows = new_slot([P, P], F32, "bias_rows")
+        nc.gpsimd.memset(bias_rows, 0.0)
+        planes = new_slot([P, KP * ROW], U8, "planes")
+        nc.vector.memset(planes.bitcast(I32), 0)
+        ident = new_slot([P, P], F32, "ident")
+        make_identity(nc, ident)
+        glow_planes = new_slot([P, KP * N], U8, "glow_planes")
+        nc.gpsimd.memset(glow_planes.bitcast(I32), 0)
 
-        nc.scalar.dma_start(tsc[0:P:4, :].bitcast(I32), tab_scales.rearrange("a q t -> q a t").bitcast(I32))
-        nc.scalar.dma_start(dsc_raw[0:P:4, :].bitcast(I32), wdust_scales.rearrange("a q c -> q a c").bitcast(I32))
-        nc.gpsimd.dma_start(rows4[0:P:4, S + H: ROW].bitcast(I32),
-                            wglow_scales.rearrange("a q c -> q a c").bitcast(I32))
-        tab = [staged([P, T], I32, "tab%d" % a, "BA"[a]) for a in range(KP)]
-        dw_raw = keep.tile([P, KP, H // 2], I32, name="dw_raw", align_bytes=64)
-        nc.sync.dma_start(tab[0][:], tab_words[0].rearrange("p t i -> p (t i)").bitcast(I32))
-        nc.sync.dma_start(dw_raw[:], wdust_words.rearrange("a p c -> p a c").bitcast(I32))
-        nc.sync.dma_start(tab[1][:], tab_words[1].rearrange("p t i -> p (t i)").bitcast(I32))
-        brows = bdust.rearrange("(b g t i) -> b t g i", b=HP, t=PACK, i=4)
+        nc.scalar.dma_start(tab_rows[0:P:ROW_STEP, :].bitcast(I32),
+                            tab_scales.rearrange("a q t -> q a t").bitcast(I32))
+        nc.scalar.dma_start(dust_rows[0:P:ROW_STEP, :].bitcast(I32),
+                            wdust_scales.rearrange("a q c -> q a c").bitcast(I32))
+        tab = [new_slot([P, T], I32, "tab%d" % a) for a in range(KP)]
+        dust_raw = new_slot([P, KP, H // 2], I32, "dust_raw")
+        nc.sync.dma_start(tab[0], tab_words[0].rearrange("p t i -> p (t i)").bitcast(I32))
+        nc.sync.dma_start(dust_raw, wdust_words.rearrange("a p c -> p a c").bitcast(I32))
+        nc.sync.dma_start(tab[1], tab_words[1].rearrange("p t i -> p (t i)").bitcast(I32))
+        bias_order = bdust.rearrange("(b g t i) -> b t g i", b=HP, t=PACK, i=RUN)
         for b in range(HP):
-            nc.gpsimd.dma_start(braw[PACK * b: PACK * (b + 1), :].rearrange("t (g i) -> t g i", i=4), brows[b])
-        ident = keep.tile([P, P], F32, name="ident")
-        make_identity(nc, ident[:])
+            nc.gpsimd.dma_start(bias_rows[PACK * b: PACK * (b + 1), :].rearrange("t (g i) -> t g i", i=RUN),
+                                bias_order[b])
+        for d in range(QUADS):
+            nc.gpsimd.dma_start(
+                glow_planes[QUAD * d: QUAD * d + BLOCKS, :].bitcast(I32).rearrange("x (a c) -> x a c", a=KP),
+                wglow_scales[:, BLOCKS * d: BLOCKS * (d + 1), :].rearrange("a x c -> x a c").bitcast(I32))
 
-        picked = keep.tile([P, S], U8, name="picked", align_bytes=64)
-        nc.vector.tensor_copy(picked[:], tsc[:].indirect(offsets[:]))
+        picked = new_slot([P, S], U8, "picked")
+        nc.vector.tensor_copy(picked, tab_rows.indirect(offsets[:]))
+        rows = new_slot([P, ROW], U8, "rows")
         nc.vector.tensor_copy(
-            rows4[:, S: S + H].bitcast(I32).rearrange("p (b t c i) -> p b c t i", b=HP, t=PACK, i=4),
-            dsc_raw[:].bitcast(I32).rearrange("p (b c i t) -> p b c t i", b=HP, t=PACK, i=4))
-        nc.vector.tensor_copy(rows4[:, 0:S].bitcast(I32), picked[:].bitcast(I32))
+            rows[:, S:ROW].bitcast(I32).rearrange("p (b t c u) -> p b c t u", b=HP, t=PACK, u=4),
+            dust_rows.bitcast(I32).rearrange("p (b c u t) -> p b c t u", b=HP, t=PACK, u=4))
+        nc.vector.tensor_copy(rows[:, 0:S].bitcast(I32), picked.bitcast(I32))
         for d in range(QUADS):
             nc.scalar.dma_start(
-                planes[32 * d: 32 * d + 4, :].bitcast(I32).rearrange("q (a j) -> q a j", a=KP),
-                rows4[32 * d: 32 * (d + 1): 4, :].bitcast(I32))
+                planes[QUAD * d: QUAD * d + BLOCKS, :].bitcast(I32).rearrange("x (a c) -> x a c", a=KP),
+                rows[QUAD * d: QUAD * (d + 1): ROW_STEP, :].bitcast(I32))
 
-        v = [staged([P, S], U32, "v0", "X"), keep.tile([P, S], U32, name="v1", align_bytes=64)]
-        nc.vector.tensor_copy(v[0][:], tab[0][:].bitcast(U32).indirect(offsets[:]))
-        dw = staged([P, 2 * KP * H], U8, "dw", "B")
+        def v_plane(a, first, width):
+            return planes[:, a * ROW + first: a * ROW + first + width]
+
+        v = [in_slot("tab_rows", [P, S], U32, "v0"), new_slot([P, S], U32, "v1")]
+        nc.vector.tensor_copy(v[0], tab[0].bitcast(U32).indirect(offsets[:]))
+        dust = in_slot("picked", [P, 2 * KP * H], U8, "dust")
         nc.vector.tensor_copy(
-            dw[:].bitcast(I32).rearrange("p (u t g w) -> p u t g w", u=KP * HP, t=PACK, w=2),
-            dw_raw[:].rearrange("p a (b g t w) -> p (a b) t g w", b=HP, t=PACK, w=2))
-        nc.vector.tensor_copy(v[1][:], tab[1][:].bitcast(U32).indirect(offsets[:]))
-        nbias = staged([P, HP, PACK], F32, "nbias", "nbias")
-        turned = bank(HP * PACK - 1, "turned")
-        nc.tensor.transpose(turned[:, 0:P], braw[:], ident[:])
-        nc.scalar.activation(nbias[:].rearrange("p b t -> p (b t)"), turned[:, 0: HP * PACK], COPY, scale=-1.0)
+            dust.bitcast(I32).rearrange("p (u t g w) -> p u t g w", u=KP * HP, t=PACK, w=2),
+            dust_raw.rearrange("p a (b g t w) -> p (a b) t g w", b=HP, t=PACK, w=2))
+        nc.vector.tensor_copy(v[1], tab[1].bitcast(U32).indirect(offsets[:]))
 
-        e = []
+        turned = bank(2 * JC - 1, "turned")
+        nc.tensor.transpose(turned[:, 0:P], bias_rows, ident)
+        minus_bias = []
         for b in range(HP):
-            eb = staged([P, PACK, S], F32, "e%d" % b, "e%d" % b)
-            e.append(eb)
+            minus_bias.append(new_slot([P, PACK], F32, "minus_bias%d" % b))
+            nc.scalar.activation(minus_bias[b], turned[:, PACK * b: PACK * (b + 1)], COPY, scale=-1.0)
+
+        def haze(b):
+            e = new_slot([P, PACK, S], F32, "e%d" % b)
             for t in range(PACK):
-                acc = bank(PACK * b + t, "d%d%d" % (b, t))
+                depth = bank(PACK * b + t, "depth%d%d" % (b, t))
                 for a in range(KP):
-                    c0 = a * H + b * PASS + t * P
-                    s0 = a * ROW + S + b * PASS + t * P
-                    nc.tensor.matmul_mx(acc[:], lhsT=dw[:, 2 * c0: 2 * (c0 + P)].bitcast(FP4X4),
-                                        lhsT_scale=planes[:, s0: s0 + P],
-                                        rhs=v[a][:].bitcast(FP8X4), rhs_scale=planes[:, a * ROW: a * ROW + S],
+                    column = b * PASS + t * P
+                    nc.tensor.matmul_mx(depth, lhsT=dust[:, 2 * (a * H + column): 2 * (a * H + column + P)].bitcast(FP4X4),
+                                        lhsT_scale=planes[:, a * ROW + S + column: a * ROW + S + column + P],
+                                        rhs=v[a].bitcast(FP8X4), rhs_scale=v_plane(a, 0, S),
                                         start=(a == 0), stop=(a == KP - 1))
-                nc.scalar.activation(eb[:, t, :], acc[:], EXP, bias=nbias[:, b, t: t + 1], scale=-1.0)
+                nc.scalar.activation(e[:, t, :], depth, EXP, bias=minus_bias[b][:, t: t + 1], scale=-1.0)
+            return e
 
         def load_wlight(a, b, slot):
-            raw = staged([P, PACK, PASS], F32, "wl%d%d" % (a, b), slot)
-            nc.sync.dma_start(raw[:], wlight[a * PASS: (a + 1) * PASS, b * PASS: (b + 1) * PASS]
+            raw = in_slot(slot, [P, PACK, PASS], F32, "wlight%d%d" % (a, b))
+            nc.sync.dma_start(raw, wlight[a * PASS: (a + 1) * PASS, b * PASS: (b + 1) * PASS]
                               .rearrange("(p j) c -> p j c", j=PACK))
-            return raw[:].rearrange("p j (g t i) -> p t g j i", t=PACK, i=4)
+            return raw.rearrange("p j (g t i) -> p t g j i", t=PACK, i=RUN)
 
-        def cast_half(grouped, src, half, copy):
-            copy(grouped.rearrange("p (t g i j) -> p t g j i", t=2, i=4, j=PACK), src[:, 2 * half: 2 * half + 2])
+        def round_half(rounded, raw, half, copy):
+            copy(rounded.rearrange("p (t g i j) -> p t g j i", t=2, i=RUN, j=PACK), raw[:, 2 * half: 2 * half + 2])
 
-        def quantise(grouped, codes, name):
-            scales = keep.tile([P, codes.shape[1]], U8, name=name, align_bytes=64)
-            nc.vector.quantize_mx(codes.bitcast(FP8X4), scales[:], grouped)
-            return codes, scales[:]
+        def quantise(rounded, codes, name):
+            scales = new_slot([P, codes.shape[1]], U8, name)
+            nc.vector.quantize_mx(codes.bitcast(FP8X4), scales, rounded)
+            return codes, scales
 
-        def light_passes(lights, a, quant):
+        def light_passes(lights, a, halves):
             for jc in range(JC):
                 for t in range(PACK):
-                    codes, scales = quant[t // 2]
-                    m = slice((t % 2) * P, (t % 2 + 1) * P)
-                    nc.tensor.matmul_mx(lights[jc][:, t * P: (t + 1) * P], lhsT=codes[:, m].bitcast(FP8X4),
-                                        lhsT_scale=scales[:, m],
+                    codes, scales = halves[t // 2]
+                    columns = slice((t % 2) * P, (t % 2 + 1) * P)
+                    nc.tensor.matmul_mx(lights[jc][:, t * P: (t + 1) * P], lhsT=codes[:, columns].bitcast(FP8X4),
+                                        lhsT_scale=scales[:, columns],
                                         rhs=v[a][:, jc * P: (jc + 1) * P].bitcast(FP8X4),
-                                        rhs_scale=planes[:, a * ROW + jc * P: a * ROW + (jc + 1) * P],
+                                        rhs_scale=v_plane(a, jc * P, P),
                                         start=(a == 0 and t == 0), stop=(a == KP - 1 and t == PACK - 1))
 
-        def dim(b, jc, light):
-            h = staged([P, PASS], BF16, "h%d%d" % (b, jc), "h%d%d" % (b, jc))
+        def dim(e, light, b, jc):
+            h = new_slot([P, PASS], BF16, "h%d%d" % (b, jc))
             nc.vector.scalar_tensor_tensor(
-                h[:].rearrange("p (j t) -> p j t", t=PACK),
-                e[b][:, :, jc * P: (jc + 1) * P].rearrange("p t j -> p j t"), 1.0,
-                light[:].rearrange("p (t j) -> p j t", t=PACK), ALU.min, ALU.mult)
+                h.rearrange("p (j t) -> p j t", t=PACK), e[:, :, jc * P: (jc + 1) * P].rearrange("p t j -> p j t"), 1.0,
+                light.rearrange("p (t j) -> p j t", t=PACK), ALU.min, ALU.mult)
             return h
 
-        on_vector, on_scalar = nc.vector.tensor_copy, nc.scalar.copy
+        def quantise_h(h, b, jc):
+            return quantise(h, new_slot([P, P], U32, "h_codes%d%d" % (b, jc)), "h_scales%d%d" % (b, jc))
 
-        def own(shape, dtype, name):
-            return staged(shape, dtype, name, name)[:]
-
-        lights0 = [bank(jc, "l0%d" % jc) for jc in range(JC)]
+        e0 = haze(0)
+        lights0 = [bank(JC + jc, "light0%d" % jc) for jc in range(JC)]
         for a in range(KP):
-            src = load_wlight(a, 0, "CD"[a])
-            halves = [own([P, 2 * PASS], BF16, "g%d0%d" % (a, half)) for half in range(2)]
+            raw = load_wlight(a, 0, ("stage", "tab0")[a])
+            rounded = [new_slot([P, PACK * HALF], BF16, "rounded%d0%d" % (a, half)) for half in range(2)]
             for half in range(2):
-                cast_half(halves[half], src, half, on_vector)
-            light_passes(lights0, a, [quantise(halves[half], own([P, 2 * P], U32, "c%d0%d" % (a, half)),
-                                               "s%d0%d" % (a, half)) for half in range(2)])
-        lights1 = [bank(JC + jc, "l1%d" % jc) for jc in range(JC)]
-        src = load_wlight(0, 1, "A")
-        g01 = staged([P, PACK * PASS], BF16, "g01", "nbias")
+                round_half(rounded[half], raw, half, nc.vector.tensor_copy)
+            light_passes(lights0, a, [quantise(rounded[half], new_slot([P, HALF], U32, "codes%d0%d" % (a, half)),
+                                               "scales%d0%d" % (a, half)) for half in range(2)])
+
+        raw01 = load_wlight(0, 1, "tab1")
+        rounded01 = in_slot("minus_bias0", [P, PACK * PASS], BF16, "rounded01")
         for half in range(2):
-            cast_half(g01[:, 2 * PASS * half: 2 * PASS * (half + 1)], src, half, on_scalar)
-        src11 = load_wlight(1, 1, "C")
-        g111 = own([P, 2 * PASS], BF16, "g111")
-        cast_half(g111, src11, 1, on_scalar)
+            round_half(rounded01[:, PACK * HALF * half: PACK * HALF * (half + 1)], raw01, half, nc.scalar.copy)
+        raw11 = load_wlight(1, 1, "stage")
+        rounded111 = in_slot("tab1", [P, PACK * HALF], BF16, "rounded111")
+        round_half(rounded111, raw11, 1, nc.scalar.copy)
 
-        h0 = [dim(0, jc, lights0[jc]) for jc in range(JC)]
-        hq0 = [quantise(h0[jc][:], own([P, P], U32, "hc0%d" % jc), "hs0%d" % jc) for jc in range(JC)]
-        light_passes(lights1, 0, [quantise(g01[:, 2 * PASS * half: 2 * PASS * (half + 1)],
-                                           staged([P, 2 * P], U32, "c01%d" % half, "h0%d" % (2 + half))[:],
-                                           "s01%d" % half) for half in range(2)])
-        g110 = staged([P, 2 * PASS], BF16, "g110", "e0")[:]
-        cast_half(g110, src11, 0, on_vector)
-        q111 = quantise(g111, own([P, 2 * P], U32, "c111"), "s111")
-        q110 = quantise(g110, own([P, 2 * P], U32, "c110"), "s110")
-        light_passes(lights1, 1, [q110, q111])
+        h0 = [dim(e0, lights0[jc], 0, jc) for jc in range(JC)]
+        e1 = haze(1)
+        lights1 = [bank(jc, "light1%d" % jc) for jc in range(JC)]
+        codes01 = in_slot("e0", [P, PASS], U32, "codes01")
+        light_passes(lights1, 0, [quantise(rounded01[:, PACK * HALF * half: PACK * HALF * (half + 1)],
+                                           codes01[:, HALF * half: HALF * (half + 1)], "scales01%d" % half)
+                                  for half in range(2)])
+        rounded110 = in_slot("minus_bias0", [P, PACK * HALF], BF16, "rounded110")
+        round_half(rounded110, raw11, 0, nc.vector.tensor_copy)
+        codes11 = in_slot("stage", [P, PASS], U32, "codes11")
+        second = quantise(rounded111, codes11[:, HALF:PASS], "scales111")
+        first = quantise(rounded110, codes11[:, 0:HALF], "scales110")
+        light_passes(lights1, 1, [first, second])
+        hq0 = [quantise_h(h0[jc], 0, jc) for jc in range(JC)]
 
-        rows = wout.rearrange("(b g t i) n -> b t g i n", b=HP, t=PACK, i=4)
-        wo_bf = staged([P, HP * NT * PASS], BF16, "wo_bf", "A")
+        wout_order = wout.rearrange("(b g t i) n -> b t g i n", b=HP, t=PACK, i=RUN)
+        wout_rounded = in_slot("minus_bias1", [P, HP * NT * PASS], BF16, "wout_rounded")
         for b in range(HP):
-            wo_raw = staged([P, PACK, N], F32, "wo_raw%d" % b, ("D", "g100")[b])
+            wout_raw = in_slot(("tab0", "rounded100")[b], [P, PACK, N], F32, "wout_raw%d" % b)
             for t in range(PACK):
-                nc.sync.dma_start(wo_raw[:, t, :], rows[b, t])
+                nc.sync.dma_start(wout_raw[:, t, :], wout_order[b, t])
             for n in range(NT):
-                u = NT * b + n
-                nc.scalar.copy(wo_bf[:, u * PASS: (u + 1) * PASS].rearrange("p (c i t) -> p c t i", i=4, t=PACK),
-                               wo_raw[:, :, n * P: (n + 1) * P].rearrange("p t (c i) -> p c t i", i=4))
-        gw = staged([P, KP, N], I32, "gw", "g101")
-        nc.sync.dma_start(gw[:], wglow_words.rearrange("a p c i -> p a (c i)").bitcast(I32))
+                piece = NT * b + n
+                nc.scalar.copy(
+                    wout_rounded[:, piece * PASS: (piece + 1) * PASS].rearrange("p (c u t) -> p c t u", u=4, t=PACK),
+                    wout_raw[:, :, n * P: (n + 1) * P].rearrange("p t (c u) -> p c t u", u=4))
+        glow = in_slot("tab1", [P, KP, N], I32, "glow")
+        nc.sync.dma_start(glow, wglow_words.rearrange("a p c i -> p a (c i)").bitcast(I32))
 
         def quantise_wout(b, slot):
-            codes = staged([P, N], U32, "woc%d" % b, slot)
-            return [quantise(wo_bf[:, (NT * b + n) * PASS: (NT * b + n + 1) * PASS], codes[:, n * P: (n + 1) * P],
-                             "wos%d%d" % (b, n)) for n in range(NT)]
+            codes = in_slot(slot, [P, N], U32, "wout_codes%d" % b)
+            return [quantise(wout_rounded[:, (NT * b + n) * PASS: (NT * b + n + 1) * PASS],
+                             codes[:, n * P: (n + 1) * P], "wout_scales%d%d" % (b, n)) for n in range(NT)]
 
-        def quantise_h1(jc):
-            return quantise(h1[jc][:], own([P, P], U32, "hc1%d" % jc), "hs1%d" % jc)
+        h1 = [dim(e1, lights1[jc], 1, jc) for jc in range(2)]
+        wq0 = quantise_wout(0, "minus_bias0")
+        hq1 = [quantise_h(h1[0], 1, 0)]
+        h1.append(dim(e1, lights1[2], 1, 2))
+        hq1.append(quantise_h(h1[1], 1, 1))
+        wq1 = quantise_wout(1, "h10")
+        h1.append(dim(e1, lights1[3], 1, 3))
+        hq1.extend([quantise_h(h1[jc], 1, jc) for jc in range(2, JC)])
 
-        h1 = [dim(1, 0, lights1[0]), dim(1, 1, lights1[1])]
-        wo = quantise_wout(0, "e0")
-        hq1 = [quantise_h1(0)]
-        h1.append(dim(1, 2, lights1[2]))
-        hq1.append(quantise_h1(1))
-        wo.extend(quantise_wout(1, "h10"))
-        h1.append(dim(1, 3, lights1[3]))
-        hq1.extend([quantise_h1(jc) for jc in (2, 3)])
+        sums = [bank(JC + jc, "sum%d" % jc) for jc in range(JC)]
 
-        sums = [bank(jc, "o%d" % jc) for jc in range(JC)]
+        def out_pass(jc, n, lhs, rhs, start, stop):
+            nc.tensor.matmul_mx(sums[jc][:, n * P: (n + 1) * P], lhsT=lhs[0].bitcast(FP8X4), lhsT_scale=lhs[1],
+                                rhs=rhs[0].bitcast(FP8X4), rhs_scale=rhs[1], start=start, stop=stop)
 
-        def out_pass(jc, n, lhs, lhs_scale, rhs, rhs_scale, start, stop):
-            nc.tensor.matmul_mx(sums[jc][:, n * P: (n + 1) * P], lhsT=lhs.bitcast(FP8X4), lhsT_scale=lhs_scale,
-                                rhs=rhs.bitcast(FP8X4), rhs_scale=rhs_scale, start=start, stop=stop)
-
-        for jc in range(JC):
-            for n in range(NT):
-                out_pass(jc, n, wo[n][0], wo[n][1], hq0[jc][0], hq0[jc][1], n == 0, False)
         for jc in range(JC):
             for a in range(KP):
                 for n in range(NT):
-                    out_pass(jc, n, gw[:, a, n * P: (n + 1) * P], planes[:, a * ROW + S + H + n * P: a * ROW + S + H + (n + 1) * P],
-                             v[a][:, jc * P: (jc + 1) * P], planes[:, a * ROW + jc * P: a * ROW + (jc + 1) * P], False, False)
+                    out_pass(jc, n,
+                             (glow[:, a, n * P: (n + 1) * P], glow_planes[:, a * N + n * P: a * N + (n + 1) * P]),
+                             (v[a][:, jc * P: (jc + 1) * P], v_plane(a, jc * P, P)), a == 0 and n == 0, False)
+        for jc in range(JC):
+            for n in range(NT):
+                out_pass(jc, n, wq0[n], hq0[jc], False, False)
         out_rows = out.rearrange("(n p) j -> p n j", p=P)
         for jc in range(JC):
             for n in range(NT):
-                out_pass(jc, n, wo[NT + n][0], wo[NT + n][1], hq1[jc][0], hq1[jc][1], False, n == NT - 1)
-            result = keep.tile([P, NT, P], F32, name="res%d" % jc)
-            evacuate = on_vector if jc == JC - 1 else on_scalar
-            evacuate(result[:].rearrange("p n j -> p (n j)"), sums[jc][:, 0:N])
-            nc.sync.dma_start(out_rows[:, :, jc * P: (jc + 1) * P], result[:])
+                out_pass(jc, n, wq1[n], hq1[jc], False, n == NT - 1)
+            result = new_slot([P, NT, P], F32, "result%d" % jc)
+            evacuate = nc.vector.tensor_copy if jc == JC - 1 else nc.scalar.copy
+            evacuate(result.rearrange("p n j -> p (n j)"), sums[jc][:, 0:N])
+            nc.sync.dma_start(out_rows[:, :, jc * P: (jc + 1) * P], result)

from contextlib import ExitStack

import concourse.mybir as mybir
from concourse.masks import make_identity

K, T, S, H, N = 1024, 2048, 512, 1024, 384
FLOPS = 2 * S * (K * H + K * H + H * N + K * N)

F32 = mybir.dt.float32
BF16 = mybir.dt.bfloat16
I32 = mybir.dt.int32
U32 = mybir.dt.uint32
U16 = mybir.dt.uint16
U8 = mybir.dt.uint8
FP8X4 = mybir.dt.float8_e4m3fn_x4
FP4X4 = mybir.dt.float4_e2m1fn_x4
EXP = mybir.ActivationFunctionType.Exp
COPY = mybir.ActivationFunctionType.Copy
ALU = mybir.AluOpType

P = 128
PACK = 4
PASS = P * PACK
RUN = 4
KP = K // PASS
HP = H // PASS
NT = N // P
JC = S // P
QUAD = 32
QUADS = P // QUAD
BLOCKS = 4
ROW_STEP = 4
ROW = S + H
HALF = PASS // 2


def tile_list_haze_sight_lines_kernel(tc, tab_words, tab_scales, offs, wdust_words, wdust_scales, bdust,
                                               wlight, wglow_words, wglow_scales, wout, out):
    nc = tc.nc
    with ExitStack() as ctx:
        keep = ctx.enter_context(tc.tile_pool(name="keep", bufs=1))
        shared = ctx.enter_context(tc.tile_pool(name="shared", bufs=1))
        psum = ctx.enter_context(tc.psum_pool(name="psum", bufs=1))

        def in_slot(slot, shape, dtype, name):
            return shared.tile(shape, dtype, name=name, tag=slot, align_bytes=64)[:]

        def new_slot(shape, dtype, name):
            return in_slot(name, shape, dtype, name)

        def bank(index, name):
            return psum.tile([P, S], F32, name=name, tag="bank%d" % index)[:]

        offsets = keep.tile([P, S // 16], U16, name="offsets")
        nc.sync.dma_start(offsets[:], offs)

        tab_rows = new_slot([P, T], U8, "tab_rows")
        nc.vector.memset(tab_rows.bitcast(I32), 0)
        dust_rows = new_slot([P, H], U8, "dust_rows")
        nc.vector.memset(dust_rows.bitcast(I32), 0)
        bias_rows = new_slot([P, P], F32, "bias_rows")
        nc.gpsimd.memset(bias_rows, 0.0)
        planes = new_slot([P, KP * ROW], U8, "planes")
        nc.vector.memset(planes.bitcast(I32), 0)
        ident = new_slot([P, P], F32, "ident")
        make_identity(nc, ident)
        glow_planes = new_slot([P, KP * N], U8, "glow_planes")
        nc.gpsimd.memset(glow_planes.bitcast(I32), 0)

        nc.scalar.dma_start(tab_rows[0:P:ROW_STEP, :].bitcast(I32),
                            tab_scales.rearrange("a q t -> q a t").bitcast(I32))
        nc.scalar.dma_start(dust_rows[0:P:ROW_STEP, :].bitcast(I32),
                            wdust_scales.rearrange("a q c -> q a c").bitcast(I32))
        tab = [new_slot([P, T], I32, "tab%d" % a) for a in range(KP)]
        dust_raw = new_slot([P, KP, H // 2], I32, "dust_raw")
        nc.sync.dma_start(tab[0], tab_words[0].rearrange("p t i -> p (t i)").bitcast(I32))
        nc.sync.dma_start(dust_raw, wdust_words.rearrange("a p c -> p a c").bitcast(I32))
        nc.sync.dma_start(tab[1], tab_words[1].rearrange("p t i -> p (t i)").bitcast(I32))
        bias_order = bdust.rearrange("(b g t i) -> b t g i", b=HP, t=PACK, i=RUN)
        for b in range(HP):
            nc.gpsimd.dma_start(bias_rows[PACK * b: PACK * (b + 1), :].rearrange("t (g i) -> t g i", i=RUN),
                                bias_order[b])
        for d in range(QUADS):
            nc.gpsimd.dma_start(
                glow_planes[QUAD * d: QUAD * d + BLOCKS, :].bitcast(I32).rearrange("x (a c) -> x a c", a=KP),
                wglow_scales[:, BLOCKS * d: BLOCKS * (d + 1), :].rearrange("a x c -> x a c").bitcast(I32))

        picked = new_slot([P, S], U8, "picked")
        nc.vector.tensor_copy(picked, tab_rows.indirect(offsets[:]))
        rows = new_slot([P, ROW], U8, "rows")
        nc.vector.tensor_copy(
            rows[:, S:ROW].bitcast(I32).rearrange("p (b t c u) -> p b c t u", b=HP, t=PACK, u=4),
            dust_rows.bitcast(I32).rearrange("p (b c u t) -> p b c t u", b=HP, t=PACK, u=4))
        nc.vector.tensor_copy(rows[:, 0:S].bitcast(I32), picked.bitcast(I32))
        for d in range(QUADS):
            nc.scalar.dma_start(
                planes[QUAD * d: QUAD * d + BLOCKS, :].bitcast(I32).rearrange("x (a c) -> x a c", a=KP),
                rows[QUAD * d: QUAD * (d + 1): ROW_STEP, :].bitcast(I32))

        def v_plane(a, first, width):
            return planes[:, a * ROW + first: a * ROW + first + width]

        v = [in_slot("tab_rows", [P, S], U32, "v0"), new_slot([P, S], U32, "v1")]
        nc.vector.tensor_copy(v[0], tab[0].bitcast(U32).indirect(offsets[:]))
        dust = in_slot("picked", [P, 2 * KP * H], U8, "dust")
        nc.vector.tensor_copy(
            dust.bitcast(I32).rearrange("p (u t g w) -> p u t g w", u=KP * HP, t=PACK, w=2),
            dust_raw.rearrange("p a (b g t w) -> p (a b) t g w", b=HP, t=PACK, w=2))
        nc.vector.tensor_copy(v[1], tab[1].bitcast(U32).indirect(offsets[:]))

        turned = bank(2 * JC - 1, "turned")
        nc.tensor.transpose(turned[:, 0:P], bias_rows, ident)
        minus_bias = []
        for b in range(HP):
            minus_bias.append(new_slot([P, PACK], F32, "minus_bias%d" % b))
            nc.scalar.activation(minus_bias[b], turned[:, PACK * b: PACK * (b + 1)], COPY, scale=-1.0)

        def haze(b):
            e = new_slot([P, PACK, S], F32, "e%d" % b)
            for t in range(PACK):
                depth = bank(PACK * b + t, "depth%d%d" % (b, t))
                for a in range(KP):
                    column = b * PASS + t * P
                    nc.tensor.matmul_mx(depth, lhsT=dust[:, 2 * (a * H + column): 2 * (a * H + column + P)].bitcast(FP4X4),
                                        lhsT_scale=planes[:, a * ROW + S + column: a * ROW + S + column + P],
                                        rhs=v[a].bitcast(FP8X4), rhs_scale=v_plane(a, 0, S),
                                        start=(a == 0), stop=(a == KP - 1))
                nc.scalar.activation(e[:, t, :], depth, EXP, bias=minus_bias[b][:, t: t + 1], scale=-1.0)
            return e

        def load_wlight(a, b, slot):
            raw = in_slot(slot, [P, PACK, PASS], F32, "wlight%d%d" % (a, b))
            nc.sync.dma_start(raw, wlight[a * PASS: (a + 1) * PASS, b * PASS: (b + 1) * PASS]
                              .rearrange("(p j) c -> p j c", j=PACK))
            return raw.rearrange("p j (g t i) -> p t g j i", t=PACK, i=RUN)

        def round_half(rounded, raw, half, copy):
            copy(rounded.rearrange("p (t g i j) -> p t g j i", t=2, i=RUN, j=PACK), raw[:, 2 * half: 2 * half + 2])

        def quantise(rounded, codes, name):
            scales = new_slot([P, codes.shape[1]], U8, name)
            nc.vector.quantize_mx(codes.bitcast(FP8X4), scales, rounded)
            return codes, scales

        def light_passes(lights, a, halves):
            for jc in range(JC):
                for t in range(PACK):
                    codes, scales = halves[t // 2]
                    columns = slice((t % 2) * P, (t % 2 + 1) * P)
                    nc.tensor.matmul_mx(lights[jc][:, t * P: (t + 1) * P], lhsT=codes[:, columns].bitcast(FP8X4),
                                        lhsT_scale=scales[:, columns],
                                        rhs=v[a][:, jc * P: (jc + 1) * P].bitcast(FP8X4),
                                        rhs_scale=v_plane(a, jc * P, P),
                                        start=(a == 0 and t == 0), stop=(a == KP - 1 and t == PACK - 1))

        def dim(e, light, b, jc):
            h = new_slot([P, PASS], BF16, "h%d%d" % (b, jc))
            nc.vector.scalar_tensor_tensor(
                h.rearrange("p (j t) -> p j t", t=PACK), e[:, :, jc * P: (jc + 1) * P].rearrange("p t j -> p j t"), 1.0,
                light.rearrange("p (t j) -> p j t", t=PACK), ALU.min, ALU.mult)
            return h

        def quantise_h(h, b, jc):
            return quantise(h, new_slot([P, P], U32, "h_codes%d%d" % (b, jc)), "h_scales%d%d" % (b, jc))

        e0 = haze(0)
        lights0 = [bank(JC + jc, "light0%d" % jc) for jc in range(JC)]
        for a in range(KP):
            raw = load_wlight(a, 0, ("stage", "tab0")[a])
            rounded = [new_slot([P, PACK * HALF], BF16, "rounded%d0%d" % (a, half)) for half in range(2)]
            for half in range(2):
                round_half(rounded[half], raw, half, nc.vector.tensor_copy)
            light_passes(lights0, a, [quantise(rounded[half], new_slot([P, HALF], U32, "codes%d0%d" % (a, half)),
                                               "scales%d0%d" % (a, half)) for half in range(2)])

        raw01 = load_wlight(0, 1, "tab1")
        rounded01 = in_slot("minus_bias0", [P, PACK * PASS], BF16, "rounded01")
        for half in range(2):
            round_half(rounded01[:, PACK * HALF * half: PACK * HALF * (half + 1)], raw01, half, nc.scalar.copy)
        raw11 = load_wlight(1, 1, "stage")
        rounded111 = in_slot("tab1", [P, PACK * HALF], BF16, "rounded111")
        round_half(rounded111, raw11, 1, nc.scalar.copy)

        h0 = [dim(e0, lights0[jc], 0, jc) for jc in range(JC)]
        e1 = haze(1)
        lights1 = [bank(jc, "light1%d" % jc) for jc in range(JC)]
        codes01 = in_slot("e0", [P, PASS], U32, "codes01")
        light_passes(lights1, 0, [quantise(rounded01[:, PACK * HALF * half: PACK * HALF * (half + 1)],
                                           codes01[:, HALF * half: HALF * (half + 1)], "scales01%d" % half)
                                  for half in range(2)])
        rounded110 = in_slot("minus_bias0", [P, PACK * HALF], BF16, "rounded110")
        round_half(rounded110, raw11, 0, nc.vector.tensor_copy)
        codes11 = in_slot("stage", [P, PASS], U32, "codes11")
        second = quantise(rounded111, codes11[:, HALF:PASS], "scales111")
        first = quantise(rounded110, codes11[:, 0:HALF], "scales110")
        light_passes(lights1, 1, [first, second])
        hq0 = [quantise_h(h0[jc], 0, jc) for jc in range(JC)]

        wout_order = wout.rearrange("(b g t i) n -> b t g i n", b=HP, t=PACK, i=RUN)
        wout_rounded = in_slot("minus_bias1", [P, HP * NT * PASS], BF16, "wout_rounded")
        for b in range(HP):
            wout_raw = in_slot(("tab0", "rounded100")[b], [P, PACK, N], F32, "wout_raw%d" % b)
            for t in range(PACK):
                nc.sync.dma_start(wout_raw[:, t, :], wout_order[b, t])
            for n in range(NT):
                piece = NT * b + n
                nc.scalar.copy(
                    wout_rounded[:, piece * PASS: (piece + 1) * PASS].rearrange("p (c u t) -> p c t u", u=4, t=PACK),
                    wout_raw[:, :, n * P: (n + 1) * P].rearrange("p t (c u) -> p c t u", u=4))
        glow = in_slot("tab1", [P, KP, N], I32, "glow")
        nc.sync.dma_start(glow, wglow_words.rearrange("a p c i -> p a (c i)").bitcast(I32))

        def quantise_wout(b, slot):
            codes = in_slot(slot, [P, N], U32, "wout_codes%d" % b)
            return [quantise(wout_rounded[:, (NT * b + n) * PASS: (NT * b + n + 1) * PASS],
                             codes[:, n * P: (n + 1) * P], "wout_scales%d%d" % (b, n)) for n in range(NT)]

        h1 = [dim(e1, lights1[jc], 1, jc) for jc in range(2)]
        wq0 = quantise_wout(0, "minus_bias0")
        hq1 = [quantise_h(h1[0], 1, 0)]
        h1.append(dim(e1, lights1[2], 1, 2))
        hq1.append(quantise_h(h1[1], 1, 1))
        wq1 = quantise_wout(1, "h10")
        h1.append(dim(e1, lights1[3], 1, 3))
        hq1.extend([quantise_h(h1[jc], 1, jc) for jc in range(2, JC)])

        sums = [bank(JC + jc, "sum%d" % jc) for jc in range(JC)]

        def out_pass(jc, n, lhs, rhs, start, stop):
            nc.tensor.matmul_mx(sums[jc][:, n * P: (n + 1) * P], lhsT=lhs[0].bitcast(FP8X4), lhsT_scale=lhs[1],
                                rhs=rhs[0].bitcast(FP8X4), rhs_scale=rhs[1], start=start, stop=stop)

        for jc in range(JC):
            for a in range(KP):
                for n in range(NT):
                    out_pass(jc, n,
                             (glow[:, a, n * P: (n + 1) * P], glow_planes[:, a * N + n * P: a * N + (n + 1) * P]),
                             (v[a][:, jc * P: (jc + 1) * P], v_plane(a, jc * P, P)), a == 0 and n == 0, False)
        for jc in range(JC):
            for n in range(NT):
                out_pass(jc, n, wq0[n], hq0[jc], False, False)
        out_rows = out.rearrange("(n p) j -> p n j", p=P)
        for jc in range(JC):
            for n in range(NT):
                out_pass(jc, n, wq1[n], hq1[jc], False, n == NT - 1)
            result = new_slot([P, NT, P], F32, "result%d" % jc)
            evacuate = nc.vector.tensor_copy if jc == JC - 1 else nc.scalar.copy
            evacuate(result.rearrange("p n j -> p (n j)"), sums[jc][:, 0:N])
            nc.sync.dma_start(out_rows[:, :, jc * P: (jc + 1) * P], result)
